import numpy as np
import ml_dtypes


def mxq(x, axis, fmt="e4m3"):
    dtype, down = {"e4m3": (ml_dtypes.float8_e4m3fn, 7), "e5m2": (ml_dtypes.float8_e5m2, 14)}[fmt]
    v = np.moveaxis(np.asarray(x, np.float32).astype(ml_dtypes.bfloat16).astype(np.float64), axis, -1)
    blocks = v.reshape(v.shape[:-1] + (-1, 32))
    amax = np.abs(blocks).max(-1, keepdims=True)
    byte = np.maximum(np.where(amax > 0, np.frexp(amax)[1] - 1 + 127, 0) - down, 1)
    scale = np.exp2(byte - 127.0)
    codes = (blocks / scale).astype(np.float32).astype(dtype).astype(np.float64)
    return np.moveaxis((codes * scale).reshape(v.shape), -1, axis)


WIDE = False


def mx_kscale(k):
    if not WIDE:
        return np.ones(k)
    levels = np.array([10, -10, 5, -5, 0])
    if k % 512:
        return np.exp2(np.random.permutation(np.resize(levels, k // 32))).repeat(32)
    a = np.empty((k // 512, 16))
    for p in range(k // 512):
        a[p, :8] = np.random.permutation(np.resize(levels, 8))
        for g in range(8):
            far = levels[np.abs(levels - a[p, g]) >= 10]
            a[p, g + 8] = far[np.random.randint(len(far))]
    return np.exp2(a.ravel()).repeat(32)


def f64(x):
    return np.asarray(x).astype(np.float64)


def striped(idx):
    return np.tile(idx.reshape(-1, 16).T, (8, 1)).astype(np.uint16)


def unstriped(offs):
    return offs[:16].T.reshape(-1).astype(np.int64)


def striped8(idx):
    return np.concatenate([x.reshape(-1, 16).T for x in idx]).astype(np.uint16)


def runs(offs, k):
    lists = np.stack([offs[16 * r : 16 * r + 16].T.reshape(-1) for r in range(8)]).astype(np.int64)
    return lists[np.arange(k) % 512 // 64]


def pack_weight(w):
    k, n = w.shape
    w = f64(np.asarray(w, np.float32).astype(ml_dtypes.bfloat16)).reshape(k // 32, 32, n)
    amax = np.abs(w).max(1)
    byte = np.clip(np.where(amax > 0, np.frexp(amax)[1] - 1 + 127 - 7, 1), 1, 254)
    scaled = (w * np.exp2(127.0 - byte)[:, None, :]).reshape(k, n).astype(np.float32)
    words = np.ascontiguousarray(scaled.reshape(k // 512, 128, 4, n).transpose(0, 1, 3, 2)).astype(ml_dtypes.float8_e4m3fn).view(np.uint8)
    return words, np.ascontiguousarray(byte.astype(np.uint8).reshape(k // 512, 16, n))


def unpack_weight(words, scales):
    g, p, n, _ = words.shape
    vals = np.ascontiguousarray(words).view(ml_dtypes.float8_e4m3fn).astype(np.float64) * np.repeat(np.exp2(scales.astype(np.float64) - 127.0), 8, axis=1)[..., None]
    return vals.transpose(0, 1, 3, 2).reshape(g * 512, n)


E2M1 = np.array([0.0, 0.5, 1.0, 1.5, 2.0, 3.0, 4.0, 6.0, -0.0, -0.5, -1.0, -1.5, -2.0, -3.0, -4.0, -6.0])


def pack_fp4(w):
    k, n = w.shape
    w = f64(np.asarray(w, np.float32).astype(ml_dtypes.bfloat16)).reshape(k // 32, 32, n)
    amax = np.abs(w).max(1)
    mant, ex = np.frexp(amax / 6.0)
    byte = np.clip(np.where(amax > 0, np.where(mant > 0.5, ex, ex - 1) + 127, 1), 1, 254)
    scaled = (w * np.exp2(127.0 - byte)[:, None, :]).reshape(k, n).astype(np.float32)
    c = np.ascontiguousarray(scaled.reshape(k // 512, 128, 4, n).transpose(0, 1, 3, 2)).astype(ml_dtypes.float4_e2m1fn).view(np.uint8) & 0xF
    words = (c[..., 0::2] | (c[..., 1::2] << 4)).reshape(k // 512, 128, 2 * n)
    return np.ascontiguousarray(words), np.ascontiguousarray(byte.astype(np.uint8).reshape(k // 512, 16, n))


def unpack_fp4(words, scales):
    g, _, n = scales.shape
    words = np.ascontiguousarray(words).reshape(g, 128, n, 2)
    nib = np.empty((g, 128, n, 4), np.uint8)
    nib[..., 0::2] = words & 0xF
    nib[..., 1::2] = words >> 4
    vals = E2M1[nib] * np.repeat(np.exp2(scales.astype(np.float64) - 127.0), 8, axis=1)[..., None]
    return vals.transpose(0, 1, 3, 2).reshape(g * 512, n)


def sigmoid(v):
    return 1.0 / (1.0 + np.exp(-np.maximum(v, -700.0)))


K, T, S, H, G = 512, 2048, 256, 512, 2048


def setup_inputs():
    n = np.random.standard_normal
    s = mx_kscale(K)[:, None]
    packed_xT = pack_weight(n((K, T)) * s)
    packed_w1 = pack_fp4(n((K, H)) / np.sqrt(K) / s)
    packed_dT = pack_weight(n((K, G)) / s)
    return {
        "x_words": packed_xT[0],
        "x_scales": packed_xT[1],
        "w1_words": packed_w1[0],
        "w1_scales": packed_w1[1],
        "sl": np.random.uniform(1.0, 2.0, (H, 1)).astype(np.float32),
        "th": (0.5 * n((H, 1))).astype(np.float32),
        "gs": (np.random.uniform(0.5, 1.5, (K, 1)) * s).astype(np.float32),
        "d_words": packed_dT[0],
        "d_scales": packed_dT[1],
        "offs": striped(np.random.permutation(T)[:S]),
        "n1": striped(np.random.permutation(S)),
        "n2": striped(np.random.permutation(S)),
        "k1": striped8(np.random.randint(0, G, (8, H))),
        "n3": striped(np.random.permutation(S)),
        "n4": striped(np.random.permutation(S)),
    }


def reference(x_words, x_scales, w1_words, w1_scales, sl, th, gs, d_words, d_scales, offs, n1, n2, k1, n3, n4):
    d_k1 = unpack_weight(d_words, d_scales)[np.arange(K)[:, None], runs(k1, K)]
    xq = unpack_weight(x_words, x_scales)[:, unstriped(offs)]
    y = unpack_fp4(w1_words, w1_scales).T @ xq
    ds = np.zeros((H, S))
    ds[:, unstriped(n1)] = y
    sg = sigmoid(f64(sl) * (ds[:, unstriped(n2)] - f64(th)))
    z = f64(gs) * (y * sg)
    h = 0.0625 * ((d_k1.T @ mxq(z, 0, "e4m3")))
    ds2 = np.zeros((H, S))
    ds2[:, unstriped(n3)] = h
    return np.maximum(h, ds2[:, unstriped(n4)])

@@ -1,0 +1,229 @@
+from contextlib import ExitStack
+
+import concourse.mybir as mybir
+
+F32 = mybir.dt.float32
+BF16 = mybir.dt.bfloat16
+I32 = mybir.dt.int32
+U32 = mybir.dt.uint32
+U16 = mybir.dt.uint16
+U8 = mybir.dt.uint8
+FP8X4 = mybir.dt.float8_e4m3fn_x4
+FP4X4 = mybir.dt.float4_e2m1fn_x4
+ALU = mybir.AluOpType
+ACT = mybir.ActivationFunctionType
+
+K, T, S, H, G = 512, 2048, 256, 512, 2048
+P = 128
+PACK = 4
+HALF = S // 2
+WIN = 2 * S
+FLOPS = 2 * K * H * S * 2
+HALVES = (slice(0, HALF), slice(HALF, S))
+WHOLE = slice(0, S)
+QUARTER = S // 4
+QUARTERS = (slice(0, QUARTER), slice(QUARTER, HALF))
+
+
+def entries(lst, c):
+    return lst[:, c.start // 16 : c.stop // 16]
+
+
+def tile_picked_denseerlrelay_none_p_kernel(
+    tc, x_words, x_scales, w1_words, w1_scales, sl, th, gs, d_words, d_scales, offs, n1, n2, k1, n3, n4, out
+):
+    nc = tc.nc
+    with ExitStack() as ctx:
+        keep = ctx.enter_context(tc.tile_pool(name="keep", bufs=1))
+        psum = ctx.enter_context(tc.psum_pool(name="psum", bufs=1))
+
+        def sb(shape, dt, name, tag=None):
+            return keep.tile(shape, dt, name=name, tag=tag or name, align_bytes=64)
+
+        offs_l = sb([P, S // 16], U16, "offs_l")
+        n1_l = sb([P, S // 16], U16, "n1_l")
+        n2_l = sb([P, S // 16], U16, "n2_l")
+        k1_l = sb([P, H // 16], U16, "k1_l")
+        n3_l = sb([P, S // 16], U16, "n3_l")
+        n4_l = sb([P, S // 16], U16, "n4_l")
+
+        xw_tab = sb([P, T], U32, "xw_tab", tag="words")
+        xs_tab = sb([P, T], U8, "xs_tab", tag="xs_slot")
+        w1w_raw = sb([P, 2 * H], U8, "w1w_raw", tag="w1_slot")
+        w1s_raw = sb([P, H], U8, "w1s_raw")
+
+        nc.vector.memset(xs_tab[:].bitcast(I32), 0)
+        nc.vector.memset(w1s_raw[:].bitcast(I32), 0)
+        nc.sync.dma_start(offs_l[:], offs)
+        nc.scalar.dma_start(w1w_raw[:].bitcast(I32), w1_words[0].bitcast(I32))
+        nc.sync.dma_start(n1_l[:], n1)
+        nc.sync.dma_start(k1_l[:], k1)
+        nc.sync.dma_start(n2_l[:], n2)
+        nc.sync.dma_start(n3_l[:], n3)
+        nc.sync.dma_start(n4_l[:], n4)
+        nc.sync.dma_start(xw_tab[:].bitcast(I32), x_words[0].rearrange("p n t -> p (n t)").bitcast(I32))
+        for q in range(4):
+            nc.scalar.dma_start(xs_tab[32 * q : 32 * q + 4, :].bitcast(I32), x_scales[0, 4 * q : 4 * q + 4, :].bitcast(I32))
+        for q in range(4):
+            eng = nc.scalar if q < 3 else nc.gpsimd
+            eng.dma_start(w1s_raw[32 * q : 32 * q + 4, :].bitcast(I32), w1_scales[0, 4 * q : 4 * q + 4, :].bitcast(I32))
+
+        w1w = sb([P, 2 * H], U8, "w1w")
+        nc.vector.tensor_copy(
+            w1w[:].rearrange("p (t m b) -> p t m b", t=PACK, b=2), w1w_raw[:].rearrange("p (m t b) -> p t m b", t=PACK, b=2)
+        )
+        ds_tab = sb([P, G], U8, "ds_tab", tag="w1_slot")
+        nc.gpsimd.memset(ds_tab[:].bitcast(I32), 0)
+        for e in range(2):
+            nc.sync.dma_start(ds_tab[e:P:16, :].bitcast(I32), d_scales[0, e:16:2, :].bitcast(I32))
+        xs = sb([P, S], U8, "xs")
+        nc.vector.tensor_copy(xs[:], xs_tab[:].indirect(offs_l[:]))
+        rows = sb([P, 3, 2 * PACK], F32, "rows", tag="xs_slot")
+        sl_t, th_t, gs_t = (rows[:, i, 0:PACK] for i in range(3))
+        for dst, src in ((sl_t, sl), (th_t, th), (gs_t, gs)):
+            nc.sync.dma_start(dst, src.rearrange("(p t) o -> p (t o)", t=PACK))
+        w1s = [sb([P, P], U8, f"w1s{t}") for t in range(PACK)]
+        xw = sb([P, S], U32, "xw")
+        nc.vector.tensor_copy(w1s[0][:], w1s_raw[:, 0:H:PACK])
+        for c in HALVES:
+            nc.vector.tensor_copy(xw[:, c], xw_tab[:].indirect(entries(offs_l, c)))
+
+        dw_tab = sb([P, G], U32, "dw_tab", tag="words")
+        nc.sync.dma_start(dw_tab[:].bitcast(I32), d_words[0].rearrange("p n t -> p (n t)").bitcast(I32))
+
+        y_ps = {}
+        ds = [sb([P, WIN], F32, f"ds{t}") for t in range(PACK)]
+        bias = sb([P, PACK], F32, "bias")
+        sg = {}
+
+        def first_product(t):
+            if t > 0:
+                nc.vector.tensor_copy(w1s[t][:], w1s_raw[:, t:H:PACK])
+            for c in HALVES if t == 0 else (WHOLE,):
+                width = c.stop - c.start
+                bank = psum.tile([P, width], F32, name=f"y{t}_{c.start}")
+                nc.tensor.matmul_mx(
+                    out=bank[:],
+                    lhsT=w1w[:, 2 * P * t : 2 * P * (t + 1)].bitcast(FP4X4),
+                    lhsT_scale=w1s[t][:],
+                    rhs=xw[:, c].bitcast(FP8X4),
+                    rhs_scale=xs[:, c],
+                    start=True,
+                    stop=True,
+                )
+                for a, hc in enumerate(HALVES):
+                    if c.start <= hc.start < c.stop:
+                        y_ps[t, a] = bank[:, hc.start - c.start : hc.stop - c.start]
+                y_sb = sb([P, width], F32, f"ysb{t}_{c.start}", tag="last_y" if t == PACK - 1 else None)
+                nc.vector.tensor_copy(y_sb[:], bank[:])
+                nc.scalar.activation(out=ds[t][:].indirect(entries(n1_l, c)), in_=y_sb[:], func=ACT.Copy)
+
+        def gate(t, a):
+            nc.scalar.activation(
+                out=sg[t, a],
+                in_=ds[t][:].indirect(entries(n2_l, HALVES[a])),
+                func=ACT.Sigmoid,
+                scale=sl_t[:, t : t + 1],
+                bias=bias[:, t : t + 1],
+            )
+
+        nc.vector.scalar_tensor_tensor(out=bias[:], in0=sl_t, scalar=-1.0, in1=th_t, op0=ALU.mult, op1=ALU.mult)
+        for t in range(PACK):
+            sg[t, 0] = sb([P, HALF], F32, f"sg{t}")[:]
+        for t in range(PACK):
+            first_product(t)
+            if t > 0:
+                gate(t - 1, 0)
+        gate(PACK - 1, 0)
+        sg_late = sb([P, PACK * HALF], F32, "sg_late", tag="last_y")
+        for t in range(PACK):
+            sg[t, 1] = sg_late[:, t * HALF : (t + 1) * HALF]
+            gate(t, 1)
+
+        ds_g = sb([P, H], U8, "ds_g")
+        nc.vector.tensor_copy(ds_g[:], ds_tab[:].indirect(k1_l[:]))
+        dsc = sb([P, H], U8, "dsc")
+        nc.vector.tensor_copy(dsc[:].bitcast(I32), ds_g[:].bitcast(I32))
+        for e in range(2):
+            nc.sync.dma_start(dsc[2 + e : P : 32, :].bitcast(I32), ds_g[16 + e : P : 32, :].bitcast(I32))
+        dw = sb([P, H], U32, "dw")
+        nc.vector.tensor_copy(dw[:], dw_tab[:].indirect(k1_l[:]))
+
+        zw = sb([P, S], U32, "zw")
+        zs = sb([P, S], U8, "zs")
+        h_sb = sb([P, PACK, S], F32, "h_sb")
+
+        def gated(dst, t, a, c):
+            lo = HALVES[a].start
+            part = slice(c.start - lo, c.stop - lo)
+            nc.vector.scalar_tensor_tensor(
+                out=dst, in0=y_ps[t, a][:, part], scalar=gs_t[:, t : t + 1], in1=sg[t, a][:, part], op0=ALU.mult, op1=ALU.mult
+            )
+
+        def second_product(dst, b, c):
+            nc.tensor.matmul_mx(
+                out=dst,
+                lhsT=dw[:, b * P : (b + 1) * P].bitcast(FP8X4),
+                lhsT_scale=dsc[:, b * P : (b + 1) * P],
+                rhs=zw[:, c].bitcast(FP8X4),
+                rhs_scale=zs[:, c],
+                start=True,
+                stop=True,
+            )
+
+        def quantise(z, c):
+            nc.vector.quantize_mx(out=zw[:, c].bitcast(FP8X4), scales=zs[:, c], in_=z.rearrange("p n t -> p (n t)"))
+
+        def leave(dst, src):
+            nc.vector.tensor_scalar(out=dst, in0=src, scalar1=0.0625, scalar2=None, op0=ALU.mult)
+
+        early, late = HALVES
+        z_early = sb([P, HALF, PACK], BF16, "z_early", tag="words")
+        for t in range(PACK - 1):
+            gated(z_early[:, :, t], t, 0, early)
+        gated(z_early[:, :, PACK - 1], PACK - 1, 0, early)
+        quantise(z_early[:], early)
+        h_first = psum.tile([P, HALF], F32, name="h_first")
+        h_early = psum.tile([P, PACK - 1, HALF], F32, name="h_early")
+        second_product(h_first[:], 0, early)
+        leave(h_sb[:, 0, early], h_first[:])
+        for b in range(1, PACK):
+            second_product(h_early[:, b - 1, :], b, early)
+        leave(h_sb[:, 1, early], h_early[:, 0, :])
+        leave(h_sb[:, 2:PACK, early], h_early[:, 1 : PACK - 1, :])
+
+        z_planes = sb([P, PACK, HALF], BF16, "z_planes", tag="words")
+        for t in range(PACK):
+            gated(z_planes[:, t, :], t, 1, late)
+        z_late = sb([P, HALF, PACK], BF16, "z_late")
+        nc.vector.tensor_copy(
+            z_late[:].rearrange("p (c i) t -> p c t i", i=PACK), z_planes[:].rearrange("p t (c i) -> p c t i", i=PACK)
+        )
+        quantise(z_late[:], late)
+        h_late = psum.tile([P, PACK, HALF], F32, name="h_late")
+        for b in range(PACK):
+            second_product(h_late[:, b, :], b, late)
+        for b in range(0, PACK, 2):
+            leave(h_sb[:, b : b + 2, late], h_late[:, b : b + 2, :])
+
+        ds2 = [sb([P, WIN], F32, f"ds2{b}") for b in range(PACK)]
+
+        def relay(b, c):
+            nc.scalar.activation(out=ds2[b][:].indirect(entries(n3_l, c)), in_=h_sb[:, b, c], func=ACT.Copy)
+
+        def fetch(b, c):
+            width = c.stop - c.start
+            got = sb([P, width], F32, f"got{b}_{c.start}")
+            nc.scalar.activation(out=got[:], in_=ds2[b][:].indirect(entries(n4_l, c)), func=ACT.Copy)
+            res = sb([P, width], F32, f"res{b}_{c.start}")
+            nc.vector.tensor_tensor(out=res[:], in0=h_sb[:, b, c], in1=got[:], op=ALU.max)
+            nc.sync.dma_start(out[b * P : (b + 1) * P, c], res[:])
+
+        for b in range(PACK):
+            relay(b, early)
+        relay(0, late)
+        for b in range(1, PACK):
+            relay(b, late)
+            fetch(b - 1, WHOLE)
+        for c in HALVES:
+            fetch(PACK - 1, c)

@@ -57,16 +57,18 @@ def tile_picked_denseerlrelay_none_p_kernel(
         nc.sync.dma_start(offs_l[:], offs)
         nc.scalar.dma_start(w1w_raw[:].bitcast(I32), w1_words[0].bitcast(I32))
         nc.sync.dma_start(n1_l[:], n1)
-        nc.sync.dma_start(k1_l[:], k1)
-        nc.sync.dma_start(n2_l[:], n2)
-        nc.sync.dma_start(n3_l[:], n3)
-        nc.sync.dma_start(n4_l[:], n4)
         nc.sync.dma_start(xw_tab[:].bitcast(I32), x_words[0].rearrange("p n t -> p (n t)").bitcast(I32))
         for q in range(4):
             nc.scalar.dma_start(xs_tab[32 * q : 32 * q + 4, :].bitcast(I32), x_scales[0, 4 * q : 4 * q + 4, :].bitcast(I32))
         for q in range(4):
-            eng = nc.scalar if q < 3 else nc.gpsimd
+            eng = nc.scalar if q < 2 else nc.gpsimd
             eng.dma_start(w1s_raw[32 * q : 32 * q + 4, :].bitcast(I32), w1_scales[0, 4 * q : 4 * q + 4, :].bitcast(I32))
+
+        nc.sync.dma_start(k1_l[:], k1)
+        warm_in = sb([P, 1], F32, "warm_in")
+        warm_out = sb([P, 1], F32, "warm_out")
+        nc.vector.memset(warm_in[:], 0.0)
+        nc.scalar.activation(out=warm_out[:], in_=warm_in[:], func=ACT.Sigmoid)
 
         w1w = sb([P, 2 * H], U8, "w1w")
         nc.vector.tensor_copy(
@@ -76,18 +78,20 @@ def tile_picked_denseerlrelay_none_p_kernel(
         nc.gpsimd.memset(ds_tab[:].bitcast(I32), 0)
         for e in range(2):
             nc.sync.dma_start(ds_tab[e:P:16, :].bitcast(I32), d_scales[0, e:16:2, :].bitcast(I32))
+        nc.sync.dma_start(n2_l[:], n2)
         xs = sb([P, S], U8, "xs")
         nc.vector.tensor_copy(xs[:], xs_tab[:].indirect(offs_l[:]))
         rows = sb([P, 3, 2 * PACK], F32, "rows", tag="xs_slot")
         sl_t, th_t, gs_t = (rows[:, i, 0:PACK] for i in range(3))
         for dst, src in ((sl_t, sl), (th_t, th), (gs_t, gs)):
             nc.sync.dma_start(dst, src.rearrange("(p t) o -> p (t o)", t=PACK))
+        nc.sync.dma_start(n3_l[:], n3)
+        nc.sync.dma_start(n4_l[:], n4)
         w1s = [sb([P, P], U8, f"w1s{t}") for t in range(PACK)]
         xw = sb([P, S], U32, "xw")
         nc.vector.tensor_copy(w1s[0][:], w1s_raw[:, 0:H:PACK])
         for c in HALVES:
             nc.vector.tensor_copy(xw[:, c], xw_tab[:].indirect(entries(offs_l, c)))
-
         dw_tab = sb([P, G], U32, "dw_tab", tag="words")
         nc.sync.dma_start(dw_tab[:].bitcast(I32), d_words[0].rearrange("p n t -> p (n t)").bitcast(I32))
 
@@ -114,7 +118,7 @@ def tile_picked_denseerlrelay_none_p_kernel(
                 for a, hc in enumerate(HALVES):
                     if c.start <= hc.start < c.stop:
                         y_ps[t, a] = bank[:, hc.start - c.start : hc.stop - c.start]
-                y_sb = sb([P, width], F32, f"ysb{t}_{c.start}", tag="last_y" if t == PACK - 1 else None)
+                y_sb = sb([P, width], F32, f"ysb{t}_{c.start}", tag="last_y" if t == PACK - 1 else f"y{t}_{c.start}_slot")
                 nc.vector.tensor_copy(y_sb[:], bank[:])
                 nc.scalar.activation(out=ds[t][:].indirect(entries(n1_l, c)), in_=y_sb[:], func=ACT.Copy)
 
@@ -140,7 +144,7 @@ def tile_picked_denseerlrelay_none_p_kernel(
             sg[t, 1] = sg_late[:, t * HALF : (t + 1) * HALF]
             gate(t, 1)
 
-        ds_g = sb([P, H], U8, "ds_g")
+        ds_g = sb([P, H], U8, "ds_g", tag="y0_0_slot")
         nc.vector.tensor_copy(ds_g[:], ds_tab[:].indirect(k1_l[:]))
         dsc = sb([P, H], U8, "dsc")
         nc.vector.tensor_copy(dsc[:].bitcast(I32), ds_g[:].bitcast(I32))

@@ -53,16 +53,15 @@ def tile_picked_denseerlrelay_none_p_kernel(
         w1s_raw = sb([P, H], U8, "w1s_raw")
 
         nc.vector.memset(xs_tab[:].bitcast(I32), 0)
-        nc.vector.memset(w1s_raw[:].bitcast(I32), 0)
+        nc.gpsimd.memset(w1s_raw[:].bitcast(I32), 0)
         nc.sync.dma_start(offs_l[:], offs)
         nc.scalar.dma_start(w1w_raw[:].bitcast(I32), w1_words[0].bitcast(I32))
         nc.sync.dma_start(n1_l[:], n1)
+        for q in range(4):
+            nc.sync.dma_start(xs_tab[32 * q : 32 * q + 4, :].bitcast(I32), x_scales[0, 4 * q : 4 * q + 4, :].bitcast(I32))
         nc.sync.dma_start(xw_tab[:].bitcast(I32), x_words[0].rearrange("p n t -> p (n t)").bitcast(I32))
         for q in range(4):
-            nc.scalar.dma_start(xs_tab[32 * q : 32 * q + 4, :].bitcast(I32), x_scales[0, 4 * q : 4 * q + 4, :].bitcast(I32))
-        for q in range(4):
-            eng = nc.scalar if q < 2 else nc.gpsimd
-            eng.dma_start(w1s_raw[32 * q : 32 * q + 4, :].bitcast(I32), w1_scales[0, 4 * q : 4 * q + 4, :].bitcast(I32))
+            nc.sync.dma_start(w1s_raw[32 * q : 32 * q + 4, :].bitcast(I32), w1_scales[0, 4 * q : 4 * q + 4, :].bitcast(I32))
 
         nc.sync.dma_start(k1_l[:], k1)
         warm_in = sb([P, 1], F32, "warm_in")
@@ -229,5 +228,5 @@ def tile_picked_denseerlrelay_none_p_kernel(
         for b in range(1, PACK):
             relay(b, late)
             fetch(b - 1, WHOLE)
-        for c in HALVES:
+        for c in (slice(0, S - QUARTER), slice(S - QUARTER, S)):
             fetch(PACK - 1, c)

from contextlib import ExitStack

import concourse.mybir as mybir

F32 = mybir.dt.float32
BF16 = mybir.dt.bfloat16
I32 = mybir.dt.int32
U32 = mybir.dt.uint32
U16 = mybir.dt.uint16
U8 = mybir.dt.uint8
FP8X4 = mybir.dt.float8_e4m3fn_x4
FP4X4 = mybir.dt.float4_e2m1fn_x4
ALU = mybir.AluOpType
ACT = mybir.ActivationFunctionType

K, T, S, H, G = 512, 2048, 256, 512, 2048
P = 128
PACK = 4
HALF = S // 2
WIN = 2 * S
FLOPS = 2 * K * H * S * 2
HALVES = (slice(0, HALF), slice(HALF, S))
WHOLE = slice(0, S)
QUARTER = S // 4
QUARTERS = (slice(0, QUARTER), slice(QUARTER, HALF))


def entries(lst, c):
    return lst[:, c.start // 16 : c.stop // 16]


def tile_picked_denseerlrelay_none_p_kernel(
    tc, x_words, x_scales, w1_words, w1_scales, sl, th, gs, d_words, d_scales, offs, n1, n2, k1, n3, n4, out
):
    nc = tc.nc
    with ExitStack() as ctx:
        keep = ctx.enter_context(tc.tile_pool(name="keep", bufs=1))
        psum = ctx.enter_context(tc.psum_pool(name="psum", bufs=1))

        def sb(shape, dt, name, tag=None):
            return keep.tile(shape, dt, name=name, tag=tag or name, align_bytes=64)

        offs_l = sb([P, S // 16], U16, "offs_l")
        n1_l = sb([P, S // 16], U16, "n1_l")
        n2_l = sb([P, S // 16], U16, "n2_l")
        k1_l = sb([P, H // 16], U16, "k1_l")
        n3_l = sb([P, S // 16], U16, "n3_l")
        n4_l = sb([P, S // 16], U16, "n4_l")

        xw_tab = sb([P, T], U32, "xw_tab", tag="words")
        xs_tab = sb([P, T], U8, "xs_tab", tag="xs_slot")
        w1w_raw = sb([P, 2 * H], U8, "w1w_raw", tag="w1_slot")
        w1s_raw = sb([P, H], U8, "w1s_raw")

        nc.vector.memset(xs_tab[:].bitcast(I32), 0)
        nc.gpsimd.memset(w1s_raw[:].bitcast(I32), 0)
        nc.sync.dma_start(offs_l[:], offs)
        nc.scalar.dma_start(w1w_raw[:].bitcast(I32), w1_words[0].bitcast(I32))
        nc.sync.dma_start(n1_l[:], n1)
        for q in range(4):
            nc.sync.dma_start(xs_tab[32 * q : 32 * q + 4, :].bitcast(I32), x_scales[0, 4 * q : 4 * q + 4, :].bitcast(I32))
        nc.sync.dma_start(xw_tab[:].bitcast(I32), x_words[0].rearrange("p n t -> p (n t)").bitcast(I32))
        for q in range(4):
            nc.sync.dma_start(w1s_raw[32 * q : 32 * q + 4, :].bitcast(I32), w1_scales[0, 4 * q : 4 * q + 4, :].bitcast(I32))

        nc.sync.dma_start(k1_l[:], k1)
        warm_in = sb([P, 1], F32, "warm_in")
        warm_out = sb([P, 1], F32, "warm_out")
        nc.vector.memset(warm_in[:], 0.0)
        nc.scalar.activation(out=warm_out[:], in_=warm_in[:], func=ACT.Sigmoid)

        w1w = sb([P, 2 * H], U8, "w1w")
        nc.vector.tensor_copy(
            w1w[:].rearrange("p (t m b) -> p t m b", t=PACK, b=2), w1w_raw[:].rearrange("p (m t b) -> p t m b", t=PACK, b=2)
        )
        ds_tab = sb([P, G], U8, "ds_tab", tag="w1_slot")
        nc.gpsimd.memset(ds_tab[:].bitcast(I32), 0)
        for e in range(2):
            nc.sync.dma_start(ds_tab[e:P:16, :].bitcast(I32), d_scales[0, e:16:2, :].bitcast(I32))
        nc.sync.dma_start(n2_l[:], n2)
        xs = sb([P, S], U8, "xs")
        nc.vector.tensor_copy(xs[:], xs_tab[:].indirect(offs_l[:]))
        rows = sb([P, 3, 2 * PACK], F32, "rows", tag="xs_slot")
        sl_t, th_t, gs_t = (rows[:, i, 0:PACK] for i in range(3))
        for dst, src in ((sl_t, sl), (th_t, th), (gs_t, gs)):
            nc.sync.dma_start(dst, src.rearrange("(p t) o -> p (t o)", t=PACK))
        nc.sync.dma_start(n3_l[:], n3)
        nc.sync.dma_start(n4_l[:], n4)
        w1s = [sb([P, P], U8, f"w1s{t}") for t in range(PACK)]
        xw = sb([P, S], U32, "xw")
        nc.vector.tensor_copy(w1s[0][:], w1s_raw[:, 0:H:PACK])
        for c in HALVES:
            nc.vector.tensor_copy(xw[:, c], xw_tab[:].indirect(entries(offs_l, c)))
        dw_tab = sb([P, G], U32, "dw_tab", tag="words")
        nc.sync.dma_start(dw_tab[:].bitcast(I32), d_words[0].rearrange("p n t -> p (n t)").bitcast(I32))

        y_ps = {}
        ds = [sb([P, WIN], F32, f"ds{t}") for t in range(PACK)]
        bias = sb([P, PACK], F32, "bias")
        sg = {}

        def first_product(t):
            if t > 0:
                nc.vector.tensor_copy(w1s[t][:], w1s_raw[:, t:H:PACK])
            for c in HALVES if t == 0 else (WHOLE,):
                width = c.stop - c.start
                bank = psum.tile([P, width], F32, name=f"y{t}_{c.start}")
                nc.tensor.matmul_mx(
                    out=bank[:],
                    lhsT=w1w[:, 2 * P * t : 2 * P * (t + 1)].bitcast(FP4X4),
                    lhsT_scale=w1s[t][:],
                    rhs=xw[:, c].bitcast(FP8X4),
                    rhs_scale=xs[:, c],
                    start=True,
                    stop=True,
                )
                for a, hc in enumerate(HALVES):
                    if c.start <= hc.start < c.stop:
                        y_ps[t, a] = bank[:, hc.start - c.start : hc.stop - c.start]
                y_sb = sb([P, width], F32, f"ysb{t}_{c.start}", tag="last_y" if t == PACK - 1 else f"y{t}_{c.start}_slot")
                nc.vector.tensor_copy(y_sb[:], bank[:])
                nc.scalar.activation(out=ds[t][:].indirect(entries(n1_l, c)), in_=y_sb[:], func=ACT.Copy)

        def gate(t, a):
            nc.scalar.activation(
                out=sg[t, a],
                in_=ds[t][:].indirect(entries(n2_l, HALVES[a])),
                func=ACT.Sigmoid,
                scale=sl_t[:, t : t + 1],
                bias=bias[:, t : t + 1],
            )

        nc.vector.scalar_tensor_tensor(out=bias[:], in0=sl_t, scalar=-1.0, in1=th_t, op0=ALU.mult, op1=ALU.mult)
        for t in range(PACK):
            sg[t, 0] = sb([P, HALF], F32, f"sg{t}")[:]
        for t in range(PACK):
            first_product(t)
            if t > 0:
                gate(t - 1, 0)
        gate(PACK - 1, 0)
        sg_late = sb([P, PACK * HALF], F32, "sg_late", tag="last_y")
        for t in range(PACK):
            sg[t, 1] = sg_late[:, t * HALF : (t + 1) * HALF]
            gate(t, 1)

        ds_g = sb([P, H], U8, "ds_g", tag="y0_0_slot")
        nc.vector.tensor_copy(ds_g[:], ds_tab[:].indirect(k1_l[:]))
        dsc = sb([P, H], U8, "dsc")
        nc.vector.tensor_copy(dsc[:].bitcast(I32), ds_g[:].bitcast(I32))
        for e in range(2):
            nc.sync.dma_start(dsc[2 + e : P : 32, :].bitcast(I32), ds_g[16 + e : P : 32, :].bitcast(I32))
        dw = sb([P, H], U32, "dw")
        nc.vector.tensor_copy(dw[:], dw_tab[:].indirect(k1_l[:]))

        zw = sb([P, S], U32, "zw")
        zs = sb([P, S], U8, "zs")
        h_sb = sb([P, PACK, S], F32, "h_sb")

        def gated(dst, t, a, c):
            lo = HALVES[a].start
            part = slice(c.start - lo, c.stop - lo)
            nc.vector.scalar_tensor_tensor(
                out=dst, in0=y_ps[t, a][:, part], scalar=gs_t[:, t : t + 1], in1=sg[t, a][:, part], op0=ALU.mult, op1=ALU.mult
            )

        def second_product(dst, b, c):
            nc.tensor.matmul_mx(
                out=dst,
                lhsT=dw[:, b * P : (b + 1) * P].bitcast(FP8X4),
                lhsT_scale=dsc[:, b * P : (b + 1) * P],
                rhs=zw[:, c].bitcast(FP8X4),
                rhs_scale=zs[:, c],
                start=True,
                stop=True,
            )

        def quantise(z, c):
            nc.vector.quantize_mx(out=zw[:, c].bitcast(FP8X4), scales=zs[:, c], in_=z.rearrange("p n t -> p (n t)"))

        def leave(dst, src):
            nc.vector.tensor_scalar(out=dst, in0=src, scalar1=0.0625, scalar2=None, op0=ALU.mult)

        early, late = HALVES
        z_early = sb([P, HALF, PACK], BF16, "z_early", tag="words")
        for t in range(PACK - 1):
            gated(z_early[:, :, t], t, 0, early)
        gated(z_early[:, :, PACK - 1], PACK - 1, 0, early)
        quantise(z_early[:], early)
        h_first = psum.tile([P, HALF], F32, name="h_first")
        h_early = psum.tile([P, PACK - 1, HALF], F32, name="h_early")
        second_product(h_first[:], 0, early)
        leave(h_sb[:, 0, early], h_first[:])
        for b in range(1, PACK):
            second_product(h_early[:, b - 1, :], b, early)
        leave(h_sb[:, 1, early], h_early[:, 0, :])
        leave(h_sb[:, 2:PACK, early], h_early[:, 1 : PACK - 1, :])

        z_planes = sb([P, PACK, HALF], BF16, "z_planes", tag="words")
        for t in range(PACK):
            gated(z_planes[:, t, :], t, 1, late)
        z_late = sb([P, HALF, PACK], BF16, "z_late")
        nc.vector.tensor_copy(
            z_late[:].rearrange("p (c i) t -> p c t i", i=PACK), z_planes[:].rearrange("p t (c i) -> p c t i", i=PACK)
        )
        quantise(z_late[:], late)
        h_late = psum.tile([P, PACK, HALF], F32, name="h_late")
        for b in range(PACK):
            second_product(h_late[:, b, :], b, late)
        for b in range(0, PACK, 2):
            leave(h_sb[:, b : b + 2, late], h_late[:, b : b + 2, :])

        ds2 = [sb([P, WIN], F32, f"ds2{b}") for b in range(PACK)]

        def relay(b, c):
            nc.scalar.activation(out=ds2[b][:].indirect(entries(n3_l, c)), in_=h_sb[:, b, c], func=ACT.Copy)

        def fetch(b, c):
            width = c.stop - c.start
            got = sb([P, width], F32, f"got{b}_{c.start}")
            nc.scalar.activation(out=got[:], in_=ds2[b][:].indirect(entries(n4_l, c)), func=ACT.Copy)
            res = sb([P, width], F32, f"res{b}_{c.start}")
            nc.vector.tensor_tensor(out=res[:], in0=h_sb[:, b, c], in1=got[:], op=ALU.max)
            nc.sync.dma_start(out[b * P : (b + 1) * P, c], res[:])

        for b in range(PACK):
            relay(b, early)
        relay(0, late)
        for b in range(1, PACK):
            relay(b, late)
            fetch(b - 1, WHOLE)
        for c in (slice(0, S - QUARTER), slice(S - QUARTER, S)):
            fetch(PACK - 1, c)
